import numpy as np
import ml_dtypes


def mxq(x, axis, fmt="e4m3"):
    dtype, down = {"e4m3": (ml_dtypes.float8_e4m3fn, 7), "e5m2": (ml_dtypes.float8_e5m2, 14)}[fmt]
    v = np.moveaxis(np.asarray(x, np.float32).astype(ml_dtypes.bfloat16).astype(np.float64), axis, -1)
    blocks = v.reshape(v.shape[:-1] + (-1, 32))
    amax = np.abs(blocks).max(-1, keepdims=True)
    byte = np.maximum(np.where(amax > 0, np.frexp(amax)[1] - 1 + 127, 0) - down, 1)
    scale = np.exp2(byte - 127.0)
    codes = (blocks / scale).astype(np.float32).astype(dtype).astype(np.float64)
    return np.moveaxis((codes * scale).reshape(v.shape), -1, axis)


WIDE = False


def mx_kscale(k):
    if not WIDE:
        return np.ones(k)
    levels = np.array([30, -30])
    if k % 512:
        return np.exp2(np.random.permutation(np.resize(levels, k // 32))).repeat(32)
    a = np.empty((k // 512, 16))
    for p in range(k // 512):
        a[p, :8] = np.random.permutation(np.resize(levels, 8))
        for g in range(8):
            far = levels[np.abs(levels - a[p, g]) >= 10]
            a[p, g + 8] = far[np.random.randint(len(far))]
    return np.exp2(a.ravel()).repeat(32)


def f64(x):
    return np.asarray(x).astype(np.float64)


def striped(idx):
    return np.tile(np.asarray(idx).reshape(-1, 16).T, (8, 1)).astype(np.uint16)


def unstriped(offs):
    return offs[:16].T.reshape(-1).astype(np.int64)


def striped8(idx):
    return np.asarray(idx).reshape(8, -1, 16).transpose(0, 2, 1).reshape(128, -1).astype(np.uint16)


def unstriped8(offs):
    return offs.reshape(8, 16, -1).transpose(0, 2, 1).reshape(8, -1).astype(np.int64)


def pick8(x, idx, run):
    r = np.arange(len(x))
    return x[r[:, None], idx[r % (8 * run) // run]]


E2M1 = np.array([0.0, 0.5, 1.0, 1.5, 2.0, 3.0, 4.0, 6.0, -0.0, -0.5, -1.0, -1.5, -2.0, -3.0, -4.0, -6.0])


def pack_weight(w, fmt):
    k, n = w.shape
    w = f64(np.asarray(w, np.float32).astype(ml_dtypes.bfloat16)).reshape(k // 32, 32, n)
    amax = np.abs(w).max(1)
    if fmt == "e4m3":
        byte = np.frexp(amax)[1] - 1 + 127 - 7
    else:
        mant, ex = np.frexp(amax / 6.0)
        byte = np.where(mant > 0.5, ex, ex - 1) + 127
    byte = np.clip(np.where(amax > 0, byte, 1), 1, 254)
    scaled = (w * np.exp2(127.0 - byte)[:, None, :]).reshape(k, n).astype(np.float32)
    by_word = np.ascontiguousarray(scaled.reshape(k // 512, 128, 4, n).transpose(0, 1, 3, 2))
    if fmt == "e4m3":
        words = by_word.astype(ml_dtypes.float8_e4m3fn).view(np.uint8)
    else:
        c = by_word.astype(ml_dtypes.float4_e2m1fn).view(np.uint8) & 0xF
        words = (c[..., 0::2] | (c[..., 1::2] << 4)).reshape(k // 512, 128, 2 * n)
    return np.ascontiguousarray(words), np.ascontiguousarray(byte.astype(np.uint8).reshape(k // 512, 16, n))


def unpack_weight(words, scales, fmt):
    g, _, n = scales.shape
    words = np.ascontiguousarray(words).reshape(g, 128, n, -1)
    if fmt == "e4m3":
        vals = words.view(ml_dtypes.float8_e4m3fn).astype(np.float64)
    else:
        nib = np.empty((g, 128, n, 4), np.uint8)
        nib[..., 0::2] = words & 0xF
        nib[..., 1::2] = words >> 4
        vals = E2M1[nib]
    vals = vals * np.repeat(np.exp2(scales.astype(np.float64) - 127.0), 8, axis=1)[..., None]
    return vals.transpose(0, 1, 3, 2).reshape(g * 512, n)


K, T, J, R, O, N = 512, 1024, 256, 512, 128, 256


def setup_inputs():
    n = np.random.standard_normal
    idx = np.random.permutation(T)[:J]
    idx2 = np.stack([np.random.permutation(J)[:O] for _ in range(8)])
    idx3 = np.random.permutation(T)[:O]
    fk = mx_kscale(K)
    fr = mx_kscale(R)
    xtp = pack_weight(n((K, T)) / fk[:, None], "e2m1")
    wp = pack_weight(n((K, R)) * 1 / np.sqrt(K) * fk[:, None] * fr, "e4m3")
    wbp = pack_weight(n((R, N)) * 1 / np.sqrt(R) / fr[:, None], "e2m1")
    wsp = pack_weight(n((K, N)) * 1 / np.sqrt(K) * fk[:, None], "e4m3")
    return {
        "xt_words": xtp[0],
        "xt_scales": xtp[1],
        "w_words": wp[0],
        "w_scales": wp[1],
        "sa": (np.random.uniform(0.5, 1.6, (R, 1))).astype(np.float32),
        "wb_words": wbp[0],
        "wb_scales": wbp[1],
        "ws_words": wsp[0],
        "ws_scales": wsp[1],
        "offs": striped(idx),
        "offs2": striped8(idx2),
        "offs3": striped(idx3),
    }


def reference(xt_words, xt_scales, w_words, w_scales, sa, wb_words, wb_scales, ws_words, ws_scales, offs, offs2, offs3):
    idx = unstriped(offs)
    idx2 = unstriped8(offs2)
    idx3 = unstriped(offs3)
    xtu = unpack_weight(xt_words, xt_scales, "e2m1")
    wu = unpack_weight(w_words, w_scales, "e4m3")
    wbu = unpack_weight(wb_words, wb_scales, "e2m1")
    wsu = unpack_weight(ws_words, ws_scales, "e4m3")
    xtidxg = xtu[:, idx]
    a = wu.T @ xtidxg
    g1 = np.maximum(a, 0.0)
    hid = pick8(g1, idx2, 64) * f64(sa)
    hidq = mxq(hid, 0, "e5m2")
    xtidx3g = xtu[:, idx3]
    y = wbu.T @ hidq + wsu.T @ xtidx3g
    return y

@@ -1,0 +1,150 @@
+from contextlib import ExitStack
+
+import concourse.mybir as mybir
+
+K, T, J, R, O, N = 512, 1024, 256, 512, 128, 256
+FLOPS = 2 * K * R * J + 2 * R * N * O + 2 * K * N * O
+
+F32 = mybir.dt.float32
+BF16 = mybir.dt.bfloat16
+I32 = mybir.dt.int32
+U32 = mybir.dt.uint32
+U16 = mybir.dt.uint16
+U8 = mybir.dt.uint8
+E4M3 = mybir.dt.float8_e4m3fn_x4
+E5M2 = mybir.dt.float8_e5m2_x4
+E2M1 = mybir.dt.float4_e2m1fn_x4
+COPY = mybir.ActivationFunctionType.Copy
+
+P = 128
+PACK = 4
+QUADS = 4
+QUAD = 32
+
+
+def load_scale_rows(queue, plane, scales):
+    for q in range(QUADS):
+        queue.dma_start(
+            out=plane[QUAD * q : QUAD * q + PACK, :].bitcast(I32),
+            in_=scales[0, PACK * q : PACK * q + PACK, :].bitcast(I32),
+        )
+
+
+def tile_list_groupshift_solo_further_plain_kernel(
+    tc, xt_words, xt_scales, w_words, w_scales, sa, wb_words, wb_scales, ws_words, ws_scales, offs, offs2, offs3, out
+):
+    nc = tc.nc
+    with ExitStack() as ctx:
+        sb = ctx.enter_context(tc.tile_pool(name="sb", bufs=1))
+        ps = ctx.enter_context(tc.psum_pool(name="ps", bufs=1))
+
+        slots = sb.tile([P, J // 16], U16, name="slots")
+        picks = sb.tile([P, O // 16], U16, name="picks")
+        shorts = sb.tile([P, O // 16], U16, name="shorts")
+        x_words = sb.tile([P, T], U16, name="x_words", align_bytes=64)
+        x_plane = sb.tile([P, T], U8, name="x_plane", align_bytes=64)
+        w_raw = sb.tile([P, R], U32, name="w_raw", align_bytes=64)
+        w_rows = sb.tile([PACK, QUADS, R // 4], I32, name="w_rows", align_bytes=64)
+        w_plane_raw = sb.tile([P, R], U8, name="w_plane_raw", align_bytes=64)
+        wb_codes = sb.tile([P, 2 * N], U8, name="wb_codes", align_bytes=64)
+        wb_plane = sb.tile([P, N], U8, name="wb_plane", align_bytes=64)
+        ws_codes = sb.tile([P, N], U32, name="ws_codes", align_bytes=64)
+        ws_plane = sb.tile([P, N], U8, name="ws_plane", align_bytes=64)
+        sa_cols = sb.tile([P, PACK], F32, name="sa_cols")
+
+        nc.vector.memset(x_plane[:, : T // 2].bitcast(I32), 0)
+        nc.gpsimd.memset(x_plane[:, T // 2 :].bitcast(I32), 0)
+        nc.vector.memset(w_plane_raw[:].bitcast(I32), 0)
+        nc.gpsimd.memset(ws_plane[:].bitcast(I32), 0)
+        nc.gpsimd.memset(wb_plane[:].bitcast(I32), 0)
+
+        nc.sync.dma_start(out=w_rows[:], in_=w_scales[0].bitcast(I32).rearrange("(q r) c -> r q c", r=PACK))
+        nc.scalar.dma_start(out=x_words[:].bitcast(I32), in_=xt_words[0].bitcast(I32))
+        nc.sync.dma_start(slots[:], offs)
+        load_scale_rows(nc.sync, x_plane, xt_scales)
+        nc.sync.dma_start(out=w_raw[:].bitcast(I32), in_=w_words[0].rearrange("p c t -> p (c t)").bitcast(I32))
+        nc.sync.dma_start(picks[:], offs2)
+        nc.sync.dma_start(out=sa_cols[:], in_=sa.rearrange("(p t) o -> p (t o)", t=PACK))
+        nc.sync.dma_start(shorts[:], offs3)
+        load_scale_rows(nc.sync, ws_plane, ws_scales)
+        nc.sync.dma_start(out=ws_codes[:].bitcast(I32), in_=ws_words[0].rearrange("p c t -> p (c t)").bitcast(I32))
+        nc.sync.dma_start(out=wb_codes[:].bitcast(I32), in_=wb_words[0].bitcast(I32))
+        load_scale_rows(nc.sync, wb_plane, wb_scales)
+
+        for q in range(QUADS):
+            nc.vector.tensor_copy(out=w_plane_raw[QUAD * q : QUAD * q + PACK, :].bitcast(I32), in_=w_rows[:, q, :])
+        w_plane = sb.tile([P, PACK, P], U8, name="w_plane", align_bytes=64)
+        w_plane_by_t = w_plane_raw[:].rearrange("p (m t) -> p t m", t=PACK)
+        for t in range(PACK):
+            nc.gpsimd.tensor_copy(out=w_plane[:, t, :], in_=w_plane_by_t[:, t, :])
+        w_codes = [sb.tile([P, 2, P], U32, name=f"w_codes{h}", align_bytes=64) for h in range(2)]
+        w_by_t = w_raw[:].rearrange("p (c i t) -> p c t i", i=4, t=PACK)
+        for h in range(2):
+            nc.scalar.copy(out=w_codes[h][:].rearrange("p t (c i) -> p c t i", i=4), in_=w_by_t[:, :, 2 * h : 2 * h + 2, :])
+
+        xg_plane = sb.tile([P, J], U8, name="xg_plane", tag="picked_plane", align_bytes=64)
+        xg_words = sb.tile([P, J], U16, name="xg_words", tag="picked_words", align_bytes=64)
+        nc.vector.tensor_copy(out=xg_plane[:], in_=x_plane[:].indirect(slots[:]))
+        nc.vector.tensor_copy(out=xg_words[:], in_=x_words[:].indirect(slots[:]))
+
+        hid = sb.tile([P, PACK, O], BF16, name="hid", align_bytes=64)
+        g1s = {}
+        for t in range(PACK):
+            a_bank = ps.tile([P, J], F32, name=f"a_bank{t}")
+            nc.tensor.matmul_mx(
+                out=a_bank[:],
+                lhsT=w_codes[t // 2][:, t % 2, :].bitcast(E4M3),
+                lhsT_scale=w_plane[:, t, :],
+                rhs=xg_words[:].bitcast(E2M1),
+                rhs_scale=xg_plane[:],
+                start=True,
+                stop=True,
+            )
+            g1 = g1s[t] = sb.tile([P, J], F32, name=f"g1_{t}", align_bytes=64)
+            nc.vector.tensor_scalar_max(out=g1[:], in0=a_bank[:], scalar1=0.0)
+            nc.scalar.activation(out=hid[:, t, :], in_=g1[:].indirect(picks[:]), func=COPY, scale=sa_cols[:, t : t + 1])
+        xs_plane = sb.tile([P, O], U8, name="xs_plane", tag="picked_plane", align_bytes=64)
+        xs_words = sb.tile([P, O], U16, name="xs_words", tag="picked_words", align_bytes=64)
+        nc.vector.tensor_copy(out=xs_words[:], in_=x_words[:].indirect(shorts[:]))
+        nc.vector.tensor_copy(out=xs_plane[:], in_=x_plane[:].indirect(shorts[:]))
+
+        y_banks = [ps.tile([P, O], F32, name=f"y_bank{h}") for h in range(2)]
+        for h in range(2):
+            cols = slice(P * h, P * (h + 1))
+            nc.tensor.matmul_mx(
+                out=y_banks[h][:],
+                lhsT=ws_codes[:, cols].bitcast(E4M3),
+                lhsT_scale=ws_plane[:, cols],
+                rhs=xs_words[:].bitcast(E2M1),
+                rhs_scale=xs_plane[:],
+                start=True,
+                stop=False,
+            )
+
+        hid_grouped = sb.tile([P, O, PACK], BF16, name="hid_grouped", align_bytes=64)
+        nc.vector.tensor_copy(
+            out=hid_grouped[:].rearrange("p (c i) t -> p c t i", i=4),
+            in_=hid[:].rearrange("p t (c i) -> p c t i", i=4),
+        )
+        hid_codes = sb.tile([P, O], U32, name="hid_codes", align_bytes=64)
+        hid_plane = sb.tile([P, O], U8, name="hid_plane", align_bytes=64)
+        nc.vector.quantize_mx(
+            out=hid_codes[:].bitcast(E5M2), scales=hid_plane[:], in_=hid_grouped[:].rearrange("p o t -> p (o t)")
+        )
+
+        for h in range(2):
+            nc.tensor.matmul_mx(
+                out=y_banks[h][:],
+                lhsT=wb_codes[:, 2 * P * h : 2 * P * (h + 1)].bitcast(E2M1),
+                lhsT_scale=wb_plane[:, P * h : P * (h + 1)],
+                rhs=hid_codes[:].bitcast(E5M2),
+                rhs_scale=hid_plane[:],
+                start=False,
+                stop=True,
+            )
+        y0 = sb.tile([P, O], F32, name="y0")
+        nc.scalar.copy(out=y0[:], in_=y_banks[0][:])
+        nc.scalar.dma_start(out=out[0:P, :], in_=y0[:])
+        y1 = sb.tile([P, O], F32, name="y1")
+        nc.vector.tensor_copy(out=y1[:], in_=y_banks[1][:])
+        nc.sync.dma_start(out=out[P : 2 * P, :], in_=y1[:])

@@ -20,6 +20,7 @@ P = 128
 PACK = 4
 QUADS = 4
 QUAD = 32
+OH = O // 2
 
 
 def load_scale_rows(queue, plane, scales):
@@ -87,7 +88,6 @@ def tile_list_groupshift_solo_further_plain_kernel(
         nc.vector.tensor_copy(out=xg_plane[:], in_=x_plane[:].indirect(slots[:]))
         nc.vector.tensor_copy(out=xg_words[:], in_=x_words[:].indirect(slots[:]))
 
-        hid = sb.tile([P, PACK, O], BF16, name="hid", align_bytes=64)
         g1s = {}
         for t in range(PACK):
             a_bank = ps.tile([P, J], F32, name=f"a_bank{t}")
@@ -102,7 +102,21 @@ def tile_list_groupshift_solo_further_plain_kernel(
             )
             g1 = g1s[t] = sb.tile([P, J], F32, name=f"g1_{t}", align_bytes=64)
             nc.vector.tensor_scalar_max(out=g1[:], in0=a_bank[:], scalar1=0.0)
-            nc.scalar.activation(out=hid[:, t, :], in_=g1[:].indirect(picks[:]), func=COPY, scale=sa_cols[:, t : t + 1])
+
+        hid = sb.tile([P, PACK * O], BF16, name="hid", align_bytes=64)
+        for t in range(PACK - 1):
+            nc.scalar.activation(
+                out=hid[:, O * t : O * (t + 1)], in_=g1s[t][:].indirect(picks[:]), func=COPY, scale=sa_cols[:, t : t + 1]
+            )
+        t = PACK - 1
+        for h in range(2):
+            nc.scalar.activation(
+                out=hid[:, O * t + OH * h : O * t + OH * (h + 1)],
+                in_=g1s[t][:].indirect(picks[:, OH // 16 * h : OH // 16 * (h + 1)]),
+                func=COPY,
+                scale=sa_cols[:, t : t + 1],
+            )
+
         xs_plane = sb.tile([P, O], U8, name="xs_plane", tag="picked_plane", align_bytes=64)
         xs_words = sb.tile([P, O], U16, name="xs_words", tag="picked_words", align_bytes=64)
         nc.vector.tensor_copy(out=xs_words[:], in_=x_words[:].indirect(shorts[:]))
@@ -121,16 +135,19 @@ def tile_list_groupshift_solo_further_plain_kernel(
                 stop=False,
             )
 
-        hid_grouped = sb.tile([P, O, PACK], BF16, name="hid_grouped", align_bytes=64)
-        nc.vector.tensor_copy(
-            out=hid_grouped[:].rearrange("p (c i) t -> p c t i", i=4),
-            in_=hid[:].rearrange("p t (c i) -> p c t i", i=4),
-        )
+        hid_grouped = sb.tile([P, O * PACK], BF16, name="hid_grouped", align_bytes=64)
         hid_codes = sb.tile([P, O], U32, name="hid_codes", align_bytes=64)
         hid_plane = sb.tile([P, O], U8, name="hid_plane", align_bytes=64)
-        nc.vector.quantize_mx(
-            out=hid_codes[:].bitcast(E5M2), scales=hid_plane[:], in_=hid_grouped[:].rearrange("p o t -> p (o t)")
-        )
+        hid_by_t = hid[:].rearrange("p (t h c i) -> p h c t i", t=PACK, h=2, i=4)
+        grouped_by_t = hid_grouped[:].rearrange("p (h c i t) -> p h c t i", h=2, i=4, t=PACK)
+        for h in range(2):
+            nc.vector.tensor_copy(out=grouped_by_t[:, h], in_=hid_by_t[:, h])
+        for h in range(2):
+            nc.vector.quantize_mx(
+                out=hid_codes[:, OH * h : OH * (h + 1)].bitcast(E5M2),
+                scales=hid_plane[:, OH * h : OH * (h + 1)],
+                in_=hid_grouped[:, OH * PACK * h : OH * PACK * (h + 1)],
+            )
 
         for h in range(2):
             nc.tensor.matmul_mx(

from contextlib import ExitStack

import concourse.mybir as mybir

K, T, J, R, O, N = 512, 1024, 256, 512, 128, 256
FLOPS = 2 * K * R * J + 2 * R * N * O + 2 * K * N * O

F32 = mybir.dt.float32
BF16 = mybir.dt.bfloat16
I32 = mybir.dt.int32
U32 = mybir.dt.uint32
U16 = mybir.dt.uint16
U8 = mybir.dt.uint8
E4M3 = mybir.dt.float8_e4m3fn_x4
E5M2 = mybir.dt.float8_e5m2_x4
E2M1 = mybir.dt.float4_e2m1fn_x4
COPY = mybir.ActivationFunctionType.Copy

P = 128
PACK = 4
QUADS = 4
QUAD = 32
OH = O // 2


def load_scale_rows(queue, plane, scales):
    for q in range(QUADS):
        queue.dma_start(
            out=plane[QUAD * q : QUAD * q + PACK, :].bitcast(I32),
            in_=scales[0, PACK * q : PACK * q + PACK, :].bitcast(I32),
        )


def tile_list_groupshift_solo_further_plain_kernel(
    tc, xt_words, xt_scales, w_words, w_scales, sa, wb_words, wb_scales, ws_words, ws_scales, offs, offs2, offs3, out
):
    nc = tc.nc
    with ExitStack() as ctx:
        sb = ctx.enter_context(tc.tile_pool(name="sb", bufs=1))
        ps = ctx.enter_context(tc.psum_pool(name="ps", bufs=1))

        slots = sb.tile([P, J // 16], U16, name="slots")
        picks = sb.tile([P, O // 16], U16, name="picks")
        shorts = sb.tile([P, O // 16], U16, name="shorts")
        x_words = sb.tile([P, T], U16, name="x_words", align_bytes=64)
        x_plane = sb.tile([P, T], U8, name="x_plane", align_bytes=64)
        w_raw = sb.tile([P, R], U32, name="w_raw", align_bytes=64)
        w_rows = sb.tile([PACK, QUADS, R // 4], I32, name="w_rows", align_bytes=64)
        w_plane_raw = sb.tile([P, R], U8, name="w_plane_raw", align_bytes=64)
        wb_codes = sb.tile([P, 2 * N], U8, name="wb_codes", align_bytes=64)
        wb_plane = sb.tile([P, N], U8, name="wb_plane", align_bytes=64)
        ws_codes = sb.tile([P, N], U32, name="ws_codes", align_bytes=64)
        ws_plane = sb.tile([P, N], U8, name="ws_plane", align_bytes=64)
        sa_cols = sb.tile([P, PACK], F32, name="sa_cols")

        nc.vector.memset(x_plane[:, : T // 2].bitcast(I32), 0)
        nc.gpsimd.memset(x_plane[:, T // 2 :].bitcast(I32), 0)
        nc.vector.memset(w_plane_raw[:].bitcast(I32), 0)
        nc.gpsimd.memset(ws_plane[:].bitcast(I32), 0)
        nc.gpsimd.memset(wb_plane[:].bitcast(I32), 0)

        nc.sync.dma_start(out=w_rows[:], in_=w_scales[0].bitcast(I32).rearrange("(q r) c -> r q c", r=PACK))
        nc.scalar.dma_start(out=x_words[:].bitcast(I32), in_=xt_words[0].bitcast(I32))
        nc.sync.dma_start(slots[:], offs)
        load_scale_rows(nc.sync, x_plane, xt_scales)
        nc.sync.dma_start(out=w_raw[:].bitcast(I32), in_=w_words[0].rearrange("p c t -> p (c t)").bitcast(I32))
        nc.sync.dma_start(picks[:], offs2)
        nc.sync.dma_start(out=sa_cols[:], in_=sa.rearrange("(p t) o -> p (t o)", t=PACK))
        nc.sync.dma_start(shorts[:], offs3)
        load_scale_rows(nc.sync, ws_plane, ws_scales)
        nc.sync.dma_start(out=ws_codes[:].bitcast(I32), in_=ws_words[0].rearrange("p c t -> p (c t)").bitcast(I32))
        nc.sync.dma_start(out=wb_codes[:].bitcast(I32), in_=wb_words[0].bitcast(I32))
        load_scale_rows(nc.sync, wb_plane, wb_scales)

        for q in range(QUADS):
            nc.vector.tensor_copy(out=w_plane_raw[QUAD * q : QUAD * q + PACK, :].bitcast(I32), in_=w_rows[:, q, :])
        w_plane = sb.tile([P, PACK, P], U8, name="w_plane", align_bytes=64)
        w_plane_by_t = w_plane_raw[:].rearrange("p (m t) -> p t m", t=PACK)
        for t in range(PACK):
            nc.gpsimd.tensor_copy(out=w_plane[:, t, :], in_=w_plane_by_t[:, t, :])
        w_codes = [sb.tile([P, 2, P], U32, name=f"w_codes{h}", align_bytes=64) for h in range(2)]
        w_by_t = w_raw[:].rearrange("p (c i t) -> p c t i", i=4, t=PACK)
        for h in range(2):
            nc.scalar.copy(out=w_codes[h][:].rearrange("p t (c i) -> p c t i", i=4), in_=w_by_t[:, :, 2 * h : 2 * h + 2, :])

        xg_plane = sb.tile([P, J], U8, name="xg_plane", tag="picked_plane", align_bytes=64)
        xg_words = sb.tile([P, J], U16, name="xg_words", tag="picked_words", align_bytes=64)
        nc.vector.tensor_copy(out=xg_plane[:], in_=x_plane[:].indirect(slots[:]))
        nc.vector.tensor_copy(out=xg_words[:], in_=x_words[:].indirect(slots[:]))

        g1s = {}
        for t in range(PACK):
            a_bank = ps.tile([P, J], F32, name=f"a_bank{t}")
            nc.tensor.matmul_mx(
                out=a_bank[:],
                lhsT=w_codes[t // 2][:, t % 2, :].bitcast(E4M3),
                lhsT_scale=w_plane[:, t, :],
                rhs=xg_words[:].bitcast(E2M1),
                rhs_scale=xg_plane[:],
                start=True,
                stop=True,
            )
            g1 = g1s[t] = sb.tile([P, J], F32, name=f"g1_{t}", align_bytes=64)
            nc.vector.tensor_scalar_max(out=g1[:], in0=a_bank[:], scalar1=0.0)

        hid = sb.tile([P, PACK * O], BF16, name="hid", align_bytes=64)
        for t in range(PACK - 1):
            nc.scalar.activation(
                out=hid[:, O * t : O * (t + 1)], in_=g1s[t][:].indirect(picks[:]), func=COPY, scale=sa_cols[:, t : t + 1]
            )
        t = PACK - 1
        for h in range(2):
            nc.scalar.activation(
                out=hid[:, O * t + OH * h : O * t + OH * (h + 1)],
                in_=g1s[t][:].indirect(picks[:, OH // 16 * h : OH // 16 * (h + 1)]),
                func=COPY,
                scale=sa_cols[:, t : t + 1],
            )

        xs_plane = sb.tile([P, O], U8, name="xs_plane", tag="picked_plane", align_bytes=64)
        xs_words = sb.tile([P, O], U16, name="xs_words", tag="picked_words", align_bytes=64)
        nc.vector.tensor_copy(out=xs_words[:], in_=x_words[:].indirect(shorts[:]))
        nc.vector.tensor_copy(out=xs_plane[:], in_=x_plane[:].indirect(shorts[:]))

        y_banks = [ps.tile([P, O], F32, name=f"y_bank{h}") for h in range(2)]
        for h in range(2):
            cols = slice(P * h, P * (h + 1))
            nc.tensor.matmul_mx(
                out=y_banks[h][:],
                lhsT=ws_codes[:, cols].bitcast(E4M3),
                lhsT_scale=ws_plane[:, cols],
                rhs=xs_words[:].bitcast(E2M1),
                rhs_scale=xs_plane[:],
                start=True,
                stop=False,
            )

        hid_grouped = sb.tile([P, O * PACK], BF16, name="hid_grouped", align_bytes=64)
        hid_codes = sb.tile([P, O], U32, name="hid_codes", align_bytes=64)
        hid_plane = sb.tile([P, O], U8, name="hid_plane", align_bytes=64)
        hid_by_t = hid[:].rearrange("p (t h c i) -> p h c t i", t=PACK, h=2, i=4)
        grouped_by_t = hid_grouped[:].rearrange("p (h c i t) -> p h c t i", h=2, i=4, t=PACK)
        for h in range(2):
            nc.vector.tensor_copy(out=grouped_by_t[:, h], in_=hid_by_t[:, h])
        for h in range(2):
            nc.vector.quantize_mx(
                out=hid_codes[:, OH * h : OH * (h + 1)].bitcast(E5M2),
                scales=hid_plane[:, OH * h : OH * (h + 1)],
                in_=hid_grouped[:, OH * PACK * h : OH * PACK * (h + 1)],
            )

        for h in range(2):
            nc.tensor.matmul_mx(
                out=y_banks[h][:],
                lhsT=wb_codes[:, 2 * P * h : 2 * P * (h + 1)].bitcast(E2M1),
                lhsT_scale=wb_plane[:, P * h : P * (h + 1)],
                rhs=hid_codes[:].bitcast(E5M2),
                rhs_scale=hid_plane[:],
                start=False,
                stop=True,
            )
        y0 = sb.tile([P, O], F32, name="y0")
        nc.scalar.copy(out=y0[:], in_=y_banks[0][:])
        nc.scalar.dma_start(out=out[0:P, :], in_=y0[:])
        y1 = sb.tile([P, O], F32, name="y1")
        nc.vector.tensor_copy(out=y1[:], in_=y_banks[1][:])
        nc.sync.dma_start(out=out[P : 2 * P, :], in_=y1[:])
